import numpy as np
import ml_dtypes


def mxq(x, axis, fmt="e4m3"):
    dtype, down = {"e4m3": (ml_dtypes.float8_e4m3fn, 7), "e5m2": (ml_dtypes.float8_e5m2, 14)}[fmt]
    v = np.moveaxis(np.asarray(x, np.float32).astype(ml_dtypes.bfloat16).astype(np.float64), axis, -1)
    blocks = v.reshape(v.shape[:-1] + (-1, 32))
    amax = np.abs(blocks).max(-1, keepdims=True)
    byte = np.maximum(np.where(amax > 0, np.frexp(amax)[1] - 1 + 127, 0) - down, 1)
    scale = np.exp2(byte - 127.0)
    codes = (blocks / scale).astype(np.float32).astype(dtype).astype(np.float64)
    return np.moveaxis((codes * scale).reshape(v.shape), -1, axis)


WIDE = False


def mx_kscale(k, group=512):
    if not WIDE:
        return np.ones(k)
    levels = np.array([18, -18])
    if group != 512:
        return np.exp2(np.random.permutation(np.resize(levels, k // group))).repeat(group)
    if k % 512:
        return np.exp2(np.random.permutation(np.resize(levels, k // 32))).repeat(32)
    a = np.empty((k // 512, 16))
    for p in range(k // 512):
        a[p, :8] = np.random.permutation(np.resize(levels, 8))
        for g in range(8):
            far = levels[np.abs(levels - a[p, g]) >= 10]
            a[p, g + 8] = far[np.random.randint(len(far))]
    return np.exp2(a.ravel()).repeat(32)


def f64(x):
    return np.asarray(x).astype(np.float64)


E2M1 = np.array([0.0, 0.5, 1.0, 1.5, 2.0, 3.0, 4.0, 6.0, -0.0, -0.5, -1.0, -1.5, -2.0, -3.0, -4.0, -6.0])


def pack_group(w):
    k, n = w.shape
    w = f64(np.asarray(w, np.float32).astype(ml_dtypes.bfloat16)).reshape(k // 32, 32, n)
    amax = np.abs(w).max(1)
    mant, ex = np.frexp(amax / 6.0)
    byte = np.clip(np.where(amax > 0, np.where(mant > 0.5, ex, ex - 1) + 127, 1), 1, 254)
    scaled = (w * np.exp2(127.0 - byte)[:, None, :]).reshape(k, n).astype(np.float32)
    c = np.ascontiguousarray(scaled.reshape(k // 4, 4, n).transpose(0, 2, 1)).astype(ml_dtypes.float4_e2m1fn).view(np.uint8) & 0xF
    return np.ascontiguousarray((c[..., 0::2] | (c[..., 1::2] << 4)).reshape(k // 4, 2 * n)), byte.astype(np.uint8)


def unpack_group(words, scales):
    p, n = words.shape[0], scales.shape[1]
    words = np.ascontiguousarray(words).reshape(p, n, 2)
    nib = np.empty((p, n, 4), np.uint8)
    nib[..., 0::2] = words & 0xF
    nib[..., 1::2] = words >> 4
    return E2M1[nib].transpose(0, 2, 1).reshape(4 * p, n) * np.repeat(np.exp2(scales.astype(np.float64) - 127.0), 32, axis=0)


def gelu(v):
    return 0.5 * v * (1.0 + np.tanh(0.7978845608028654 * (v + 0.044715 * v ** 3)))


G, D, M, N = 4, 128, 256, 1024


def setup_inputs():
    n = np.random.standard_normal
    s = mx_kscale(D, 0)[:, None]
    w_ = [pack_group(w) for w in n((G, D, M)) / np.sqrt(D) / s]
    return {
        "x": (n((G, D, N)) * s).astype(np.float32),
        "w_words": np.stack([w[0] for w in w_]),
        "w_scales": np.stack([w[1] for w in w_]),
        "r": n((G, M, N)).astype(np.float32),
    }


def reference(x, w_words, w_scales, r):
    xq = mxq(f64(x), 1, "e4m3")
    y = np.stack([unpack_group(w_words[g], w_scales[g]) for g in range(G)]).transpose(0, 2, 1) @ xq
    y = gelu(y)
    y = y + f64(r)
    return y

@@ -1,0 +1,113 @@
+from contextlib import ExitStack
+
+import concourse.mybir as mybir
+
+G, D, M, N = 4, 128, 256, 1024
+FLOPS = 2 * G * D * M * N
+
+F32 = mybir.dt.float32
+BF16 = mybir.dt.bfloat16
+I32 = mybir.dt.int32
+U32 = mybir.dt.uint32
+U8 = mybir.dt.uint8
+FP8X4 = mybir.dt.float8_e4m3fn_x4
+FP4X4 = mybir.dt.float4_e2m1fn_x4
+GELU = mybir.ActivationFunctionType.Gelu_apprx_tanh
+
+P = 128
+PACK = 4
+ROWS = D // PACK
+BLOCKS = D // 32
+N_TILE = 512
+HALVES = N // N_TILE
+PAIR = M // P
+WORD_BYTES = 2
+
+
+def tile_rows_glin_gelu_res_kernel(tc, x, w_words, w_scales, r, out):
+    nc = tc.nc
+    with ExitStack() as ctx:
+        sb = ctx.enter_context(tc.tile_pool(name="sb", bufs=1))
+        psum = ctx.enter_context(tc.psum_pool(name="psum", bufs=1))
+        ctx.enter_context(tc.manual_schedule())
+
+        x_raw = [sb.tile([P, PACK, N_TILE], F32, name="x_raw%d" % h) for h in range(HALVES)]
+        x_bf = [sb.tile([P, N_TILE, PACK], BF16, name="x_bf%d" % h, align_bytes=64) for h in range(HALVES)]
+        x_codes = [sb.tile([P, N_TILE], U32, name="x_codes%d" % h, align_bytes=64) for h in range(HALVES)]
+        x_scales = [sb.tile([P, N_TILE], U8, name="x_scales%d" % h, align_bytes=64) for h in range(HALVES)]
+        w_raw = sb.tile([P, M * WORD_BYTES], U8, align_bytes=64)
+        ws_raw = sb.tile([P, M], U8, align_bytes=64)
+        w_dealt = sb.tile([P, M * WORD_BYTES], U8, align_bytes=64)
+        ws_dealt = sb.tile([P, M], U8, align_bytes=64)
+        res = [sb.tile([P, PAIR, N], F32, name="res%d" % g) for g in range(G)]
+        y = [sb.tile([P, PAIR, N], F32, name="y%d" % g) for g in range(G)]
+        acc = [[psum.tile([P, N_TILE], F32, name="acc%d_%d" % (g, t)) for t in range(PAIR)] for g in range(G)]
+
+        x_rows = x.rearrange("g (p j) n -> (g p) j n", j=PACK)
+        for h in range(HALVES):
+            nc.sync.dma_start(out=x_raw[h][:], in_=x_rows[:, :, h * N_TILE : (h + 1) * N_TILE])
+        for g in range(G):
+            nc.sync.dma_start(
+                out=res[g][:].rearrange("p t n -> p (t n)"),
+                in_=r[g].rearrange("(p t) n -> p (t n)", t=PAIR),
+            )
+
+        nc.gpsimd.memset(ws_raw[:].bitcast(I32), 0)
+        nc.scalar.dma_start(out=w_raw[:].bitcast(I32), in_=w_words.rearrange("g p b -> (g p) b").bitcast(I32))
+        for g in range(G):
+            nc.scalar.dma_start(
+                out=ws_raw[ROWS * g : ROWS * g + BLOCKS, :].bitcast(I32), in_=w_scales[g].bitcast(I32)
+            )
+
+        nc.vector.tensor_copy(
+            out=w_dealt[:].rearrange("p (t m b) -> p t m b", t=PAIR, b=WORD_BYTES),
+            in_=w_raw[:].rearrange("p (m t b) -> p t m b", t=PAIR, b=WORD_BYTES),
+        )
+        nc.vector.tensor_copy(
+            out=ws_dealt[:].rearrange("p (t m) -> p t m", t=PAIR),
+            in_=ws_raw[:].rearrange("p (m t) -> p t m", t=PAIR),
+        )
+
+        for h in range(HALVES):
+            nc.vector.tensor_copy(out=x_bf[h][:], in_=x_raw[h][:].rearrange("p j n -> p n j"))
+            nc.vector.quantize_mx(
+                out=x_codes[h][:].bitcast(FP8X4),
+                scales=x_scales[h][:],
+                in_=x_bf[h][:].rearrange("p n j -> p (n j)"),
+            )
+
+        def multiply(g, t, h):
+            rows = slice(ROWS * g, ROWS * (g + 1))
+            nc.tensor.matmul_mx(
+                out=acc[g][t][:],
+                lhsT=w_dealt[rows, t * P * WORD_BYTES : (t + 1) * P * WORD_BYTES].bitcast(FP4X4),
+                lhsT_scale=ws_dealt[rows, t * P : (t + 1) * P],
+                rhs=x_codes[h][rows, :].bitcast(FP8X4),
+                rhs_scale=x_scales[h][rows, :],
+                start=True,
+                stop=True,
+            )
+
+        def activate(g, t, h):
+            nc.scalar.activation(out=y[g][:, t, h * N_TILE : (h + 1) * N_TILE], in_=acc[g][t][:], func=GELU)
+
+        for g in range(G):
+            for t in range(PAIR):
+                multiply(g, t, 0)
+        for g0 in range(0, G, 2):
+            for h in range(HALVES):
+                for g in (g0, g0 + 1):
+                    for t in range(PAIR):
+                        if h > 0:
+                            multiply(g, t, h)
+                        activate(g, t, h)
+
+        for g in range(G):
+            for h in range(HALVES):
+                for t in range(PAIR):
+                    cols = slice(h * N_TILE, (h + 1) * N_TILE)
+                    nc.vector.tensor_add(out=y[g][:, t, cols], in0=y[g][:, t, cols], in1=res[g][:, t, cols])
+            nc.sync.dma_start(
+                out=out[g].rearrange("(p t) n -> p (t n)", t=PAIR),
+                in_=y[g][:].rearrange("p t n -> p (t n)"),
+            )

@@ -44,21 +44,35 @@ def tile_rows_glin_gelu_res_kernel(tc, x, w_words, w_scales, r, out):
         acc = [[psum.tile([P, N_TILE], F32, name="acc%d_%d" % (g, t)) for t in range(PAIR)] for g in range(G)]
 
         x_rows = x.rearrange("g (p j) n -> (g p) j n", j=PACK)
-        for h in range(HALVES):
+
+        def load_x(h):
             nc.sync.dma_start(out=x_raw[h][:], in_=x_rows[:, :, h * N_TILE : (h + 1) * N_TILE])
+
+        nc.gpsimd.memset(ws_raw[:].bitcast(I32), 0)
+        load_x(0)
+        nc.sync.dma_start(out=w_raw[:].bitcast(I32), in_=w_words.rearrange("g p b -> (g p) b").bitcast(I32))
+        for g in range(G):
+            nc.sync.dma_start(
+                out=ws_raw[ROWS * g : ROWS * g + BLOCKS, :].bitcast(I32), in_=w_scales[g].bitcast(I32)
+            )
+        load_x(1)
         for g in range(G):
             nc.sync.dma_start(
                 out=res[g][:].rearrange("p t n -> p (t n)"),
                 in_=r[g].rearrange("(p t) n -> p (t n)", t=PAIR),
             )
 
-        nc.gpsimd.memset(ws_raw[:].bitcast(I32), 0)
-        nc.scalar.dma_start(out=w_raw[:].bitcast(I32), in_=w_words.rearrange("g p b -> (g p) b").bitcast(I32))
-        for g in range(G):
-            nc.scalar.dma_start(
-                out=ws_raw[ROWS * g : ROWS * g + BLOCKS, :].bitcast(I32), in_=w_scales[g].bitcast(I32)
+        def interleave(h):
+            nc.vector.tensor_copy(out=x_bf[h][:], in_=x_raw[h][:].rearrange("p j n -> p n j"))
+
+        def quantize(h):
+            nc.vector.quantize_mx(
+                out=x_codes[h][:].bitcast(FP8X4),
+                scales=x_scales[h][:],
+                in_=x_bf[h][:].rearrange("p n j -> p (n j)"),
             )
 
+        interleave(0)
         nc.vector.tensor_copy(
             out=w_dealt[:].rearrange("p (t m b) -> p t m b", t=PAIR, b=WORD_BYTES),
             in_=w_raw[:].rearrange("p (m t b) -> p t m b", t=PAIR, b=WORD_BYTES),
@@ -67,14 +81,9 @@ def tile_rows_glin_gelu_res_kernel(tc, x, w_words, w_scales, r, out):
             out=ws_dealt[:].rearrange("p (t m) -> p t m", t=PAIR),
             in_=ws_raw[:].rearrange("p (m t) -> p t m", t=PAIR),
         )
-
-        for h in range(HALVES):
-            nc.vector.tensor_copy(out=x_bf[h][:], in_=x_raw[h][:].rearrange("p j n -> p n j"))
-            nc.vector.quantize_mx(
-                out=x_codes[h][:].bitcast(FP8X4),
-                scales=x_scales[h][:],
-                in_=x_bf[h][:].rearrange("p n j -> p (n j)"),
-            )
+        quantize(0)
+        interleave(1)
+        quantize(1)
 
         def multiply(g, t, h):
             rows = slice(ROWS * g, ROWS * (g + 1))
@@ -91,15 +100,11 @@ def tile_rows_glin_gelu_res_kernel(tc, x, w_words, w_scales, r, out):
         def activate(g, t, h):
             nc.scalar.activation(out=y[g][:, t, h * N_TILE : (h + 1) * N_TILE], in_=acc[g][t][:], func=GELU)
 
-        for g in range(G):
-            for t in range(PAIR):
-                multiply(g, t, 0)
         for g0 in range(0, G, 2):
             for h in range(HALVES):
                 for g in (g0, g0 + 1):
                     for t in range(PAIR):
-                        if h > 0:
-                            multiply(g, t, h)
+                        multiply(g, t, h)
                         activate(g, t, h)
 
         for g in range(G):

@@ -22,6 +22,7 @@ N_TILE = 512
 HALVES = N // N_TILE
 PAIR = M // P
 WORD_BYTES = 2
+VECTOR_COLS = (344, 224)
 
 
 def tile_rows_glin_gelu_res_kernel(tc, x, w_words, w_scales, r, out):
@@ -31,7 +32,7 @@ def tile_rows_glin_gelu_res_kernel(tc, x, w_words, w_scales, r, out):
         psum = ctx.enter_context(tc.psum_pool(name="psum", bufs=1))
         ctx.enter_context(tc.manual_schedule())
 
-        x_raw = [sb.tile([P, PACK, N_TILE], F32, name="x_raw%d" % h) for h in range(HALVES)]
+        x_raw = sb.tile([P, PACK, N], F32)
         x_bf = [sb.tile([P, N_TILE, PACK], BF16, name="x_bf%d" % h, align_bytes=64) for h in range(HALVES)]
         x_codes = [sb.tile([P, N_TILE], U32, name="x_codes%d" % h, align_bytes=64) for h in range(HALVES)]
         x_scales = [sb.tile([P, N_TILE], U8, name="x_scales%d" % h, align_bytes=64) for h in range(HALVES)]
@@ -39,23 +40,23 @@ def tile_rows_glin_gelu_res_kernel(tc, x, w_words, w_scales, r, out):
         ws_raw = sb.tile([P, M], U8, align_bytes=64)
         w_dealt = sb.tile([P, M * WORD_BYTES], U8, align_bytes=64)
         ws_dealt = sb.tile([P, M], U8, align_bytes=64)
+        zero = sb.tile([P, 1], F32)
+        bias = sb.tile([P, 1], F32)
         res = [sb.tile([P, PAIR, N], F32, name="res%d" % g) for g in range(G)]
         y = [sb.tile([P, PAIR, N], F32, name="y%d" % g) for g in range(G)]
         acc = [[psum.tile([P, N_TILE], F32, name="acc%d_%d" % (g, t)) for t in range(PAIR)] for g in range(G)]
 
-        x_rows = x.rearrange("g (p j) n -> (g p) j n", j=PACK)
-
-        def load_x(h):
-            nc.sync.dma_start(out=x_raw[h][:], in_=x_rows[:, :, h * N_TILE : (h + 1) * N_TILE])
-
         nc.gpsimd.memset(ws_raw[:].bitcast(I32), 0)
-        load_x(0)
+        nc.vector.memset(zero[:], 0.0)
+        nc.scalar.activation(out=bias[:], in_=zero[:], func=GELU)
         nc.sync.dma_start(out=w_raw[:].bitcast(I32), in_=w_words.rearrange("g p b -> (g p) b").bitcast(I32))
+        nc.sync.dma_start(
+            out=x_raw[:].rearrange("p j n -> p (j n)"), in_=x.rearrange("g (p j) n -> (g p) (j n)", j=PACK)
+        )
         for g in range(G):
             nc.sync.dma_start(
                 out=ws_raw[ROWS * g : ROWS * g + BLOCKS, :].bitcast(I32), in_=w_scales[g].bitcast(I32)
             )
-        load_x(1)
         for g in range(G):
             nc.sync.dma_start(
                 out=res[g][:].rearrange("p t n -> p (t n)"),
@@ -63,7 +64,10 @@ def tile_rows_glin_gelu_res_kernel(tc, x, w_words, w_scales, r, out):
             )
 
         def interleave(h):
-            nc.vector.tensor_copy(out=x_bf[h][:], in_=x_raw[h][:].rearrange("p j n -> p n j"))
+            split = VECTOR_COLS[h]
+            source = x_raw[:, :, h * N_TILE : (h + 1) * N_TILE].rearrange("p j n -> p n j")
+            nc.vector.tensor_copy(out=x_bf[h][:, :split, :], in_=source[:, :split, :])
+            nc.scalar.copy(out=x_bf[h][:, split:, :], in_=source[:, split:, :])
 
         def quantize(h):
             nc.vector.quantize_mx(
@@ -72,11 +76,11 @@ def tile_rows_glin_gelu_res_kernel(tc, x, w_words, w_scales, r, out):
                 in_=x_bf[h][:].rearrange("p n j -> p (n j)"),
             )
 
-        interleave(0)
         nc.vector.tensor_copy(
             out=w_dealt[:].rearrange("p (t m b) -> p t m b", t=PAIR, b=WORD_BYTES),
             in_=w_raw[:].rearrange("p (m t b) -> p t m b", t=PAIR, b=WORD_BYTES),
         )
+        interleave(0)
         nc.vector.tensor_copy(
             out=ws_dealt[:].rearrange("p (t m) -> p t m", t=PAIR),
             in_=ws_raw[:].rearrange("p (m t) -> p t m", t=PAIR),
@@ -98,7 +102,17 @@ def tile_rows_glin_gelu_res_kernel(tc, x, w_words, w_scales, r, out):
             )
 
         def activate(g, t, h):
-            nc.scalar.activation(out=y[g][:, t, h * N_TILE : (h + 1) * N_TILE], in_=acc[g][t][:], func=GELU)
+            nc.scalar.activation(out=y[g][:, t, h * N_TILE : (h + 1) * N_TILE], in_=acc[g][t][:], func=GELU, bias=bias[:])
+
+        def add_residual(g, t, h):
+            cols = slice(h * N_TILE, (h + 1) * N_TILE)
+            nc.vector.tensor_add(out=y[g][:, t, cols], in0=y[g][:, t, cols], in1=res[g][:, t, cols])
+
+        def store(g):
+            nc.sync.dma_start(
+                out=out[g].rearrange("(p t) n -> p (t n)", t=PAIR),
+                in_=y[g][:].rearrange("p t n -> p (t n)"),
+            )
 
         for g0 in range(0, G, 2):
             for h in range(HALVES):
@@ -106,13 +120,6 @@ def tile_rows_glin_gelu_res_kernel(tc, x, w_words, w_scales, r, out):
                     for t in range(PAIR):
                         multiply(g, t, h)
                         activate(g, t, h)
-
-        for g in range(G):
-            for h in range(HALVES):
-                for t in range(PAIR):
-                    cols = slice(h * N_TILE, (h + 1) * N_TILE)
-                    nc.vector.tensor_add(out=y[g][:, t, cols], in0=y[g][:, t, cols], in1=res[g][:, t, cols])
-            nc.sync.dma_start(
-                out=out[g].rearrange("(p t) n -> p (t n)", t=PAIR),
-                in_=y[g][:].rearrange("p t n -> p (t n)"),
-            )
+                        add_residual(g, t, h)
+                    if h == HALVES - 1:
+                        store(g)

@@ -22,7 +22,7 @@ N_TILE = 512
 HALVES = N // N_TILE
 PAIR = M // P
 WORD_BYTES = 2
-VECTOR_COLS = (344, 224)
+RUN = 4
 
 
 def tile_rows_glin_gelu_res_kernel(tc, x, w_words, w_scales, r, out):
@@ -33,7 +33,7 @@ def tile_rows_glin_gelu_res_kernel(tc, x, w_words, w_scales, r, out):
         ctx.enter_context(tc.manual_schedule())
 
         x_raw = sb.tile([P, PACK, N], F32)
-        x_bf = [sb.tile([P, N_TILE, PACK], BF16, name="x_bf%d" % h, align_bytes=64) for h in range(HALVES)]
+        x_bf = sb.tile([P, N * PACK], BF16, align_bytes=64)
         x_codes = [sb.tile([P, N_TILE], U32, name="x_codes%d" % h, align_bytes=64) for h in range(HALVES)]
         x_scales = [sb.tile([P, N_TILE], U8, name="x_scales%d" % h, align_bytes=64) for h in range(HALVES)]
         w_raw = sb.tile([P, M * WORD_BYTES], U8, align_bytes=64)
@@ -46,48 +46,58 @@ def tile_rows_glin_gelu_res_kernel(tc, x, w_words, w_scales, r, out):
         y = [sb.tile([P, PAIR, N], F32, name="y%d" % g) for g in range(G)]
         acc = [[psum.tile([P, N_TILE], F32, name="acc%d_%d" % (g, t)) for t in range(PAIR)] for g in range(G)]
 
-        nc.gpsimd.memset(ws_raw[:].bitcast(I32), 0)
-        nc.vector.memset(zero[:], 0.0)
-        nc.scalar.activation(out=bias[:], in_=zero[:], func=GELU)
-        nc.sync.dma_start(out=w_raw[:].bitcast(I32), in_=w_words.rearrange("g p b -> (g p) b").bitcast(I32))
-        nc.sync.dma_start(
-            out=x_raw[:].rearrange("p j n -> p (j n)"), in_=x.rearrange("g (p j) n -> (g p) (j n)", j=PACK)
-        )
-        for g in range(G):
+        def load_scales():
+            for g in range(G):
+                nc.sync.dma_start(
+                    out=ws_raw[ROWS * g : ROWS * g + BLOCKS, :].bitcast(I32), in_=w_scales[g].bitcast(I32)
+                )
+
+        def load_words():
+            nc.sync.dma_start(out=w_raw[:].bitcast(I32), in_=w_words.rearrange("g p b -> (g p) b").bitcast(I32))
+
+        def load_x():
             nc.sync.dma_start(
-                out=ws_raw[ROWS * g : ROWS * g + BLOCKS, :].bitcast(I32), in_=w_scales[g].bitcast(I32)
+                out=x_raw[:].rearrange("p j n -> p (j n)"), in_=x.rearrange("g (p j) n -> (g p) (j n)", j=PACK)
             )
-        for g in range(G):
+
+        def load_res(g):
             nc.sync.dma_start(
                 out=res[g][:].rearrange("p t n -> p (t n)"),
                 in_=r[g].rearrange("(p t) n -> p (t n)", t=PAIR),
             )
 
-        def interleave(h):
-            split = VECTOR_COLS[h]
-            source = x_raw[:, :, h * N_TILE : (h + 1) * N_TILE].rearrange("p j n -> p n j")
-            nc.vector.tensor_copy(out=x_bf[h][:, :split, :], in_=source[:, :split, :])
-            nc.scalar.copy(out=x_bf[h][:, split:, :], in_=source[:, split:, :])
+        def views(lo, hi):
+            target = x_bf[:, lo * PACK : hi * PACK].rearrange("p (c i j) -> p c j i", i=RUN, j=PACK)
+            source = x_raw[:, :, lo:hi].rearrange("p j (c i) -> p c j i", i=RUN)
+            return target, source
 
-        def quantize(h):
+        def interleave_vector(lo, hi):
+            target, source = views(lo, hi)
+            nc.vector.tensor_copy(out=target, in_=source)
+
+        def interleave_scalar(lo, hi):
+            target, source = views(lo, hi)
+            nc.scalar.copy(out=target, in_=source)
+
+        def quantize(lo, hi):
+            h, at = divmod(lo, N_TILE)
             nc.vector.quantize_mx(
-                out=x_codes[h][:].bitcast(FP8X4),
-                scales=x_scales[h][:],
-                in_=x_bf[h][:].rearrange("p n j -> p (n j)"),
+                out=x_codes[h][:, at : at + hi - lo].bitcast(FP8X4),
+                scales=x_scales[h][:, at : at + hi - lo],
+                in_=x_bf[:, lo * PACK : hi * PACK],
             )
 
-        nc.vector.tensor_copy(
-            out=w_dealt[:].rearrange("p (t m b) -> p t m b", t=PAIR, b=WORD_BYTES),
-            in_=w_raw[:].rearrange("p (m t b) -> p t m b", t=PAIR, b=WORD_BYTES),
-        )
-        interleave(0)
-        nc.vector.tensor_copy(
-            out=ws_dealt[:].rearrange("p (t m) -> p t m", t=PAIR),
-            in_=ws_raw[:].rearrange("p (m t) -> p t m", t=PAIR),
-        )
-        quantize(0)
-        interleave(1)
-        quantize(1)
+        def deal_words():
+            nc.vector.tensor_copy(
+                out=w_dealt[:].rearrange("p (t m b) -> p t m b", t=PAIR, b=WORD_BYTES),
+                in_=w_raw[:].rearrange("p (m t b) -> p t m b", t=PAIR, b=WORD_BYTES),
+            )
+
+        def deal_scales():
+            nc.vector.tensor_copy(
+                out=ws_dealt[:].rearrange("p (t m) -> p t m", t=PAIR),
+                in_=ws_raw[:].rearrange("p (m t) -> p t m", t=PAIR),
+            )
 
         def multiply(g, t, h):
             rows = slice(ROWS * g, ROWS * (g + 1))
@@ -101,12 +111,12 @@ def tile_rows_glin_gelu_res_kernel(tc, x, w_words, w_scales, r, out):
                 stop=True,
             )
 
-        def activate(g, t, h):
-            nc.scalar.activation(out=y[g][:, t, h * N_TILE : (h + 1) * N_TILE], in_=acc[g][t][:], func=GELU, bias=bias[:])
-
-        def add_residual(g, t, h):
-            cols = slice(h * N_TILE, (h + 1) * N_TILE)
-            nc.vector.tensor_add(out=y[g][:, t, cols], in0=y[g][:, t, cols], in1=res[g][:, t, cols])
+        def finish(g, t, h, pieces):
+            width = N_TILE // pieces
+            for at in range(0, N_TILE, width):
+                cols = slice(h * N_TILE + at, h * N_TILE + at + width)
+                nc.scalar.activation(out=y[g][:, t, cols], in_=acc[g][t][:, at : at + width], func=GELU, bias=bias[:])
+                nc.vector.tensor_add(out=y[g][:, t, cols], in0=y[g][:, t, cols], in1=res[g][:, t, cols])
 
         def store(g):
             nc.sync.dma_start(
@@ -114,12 +124,33 @@ def tile_rows_glin_gelu_res_kernel(tc, x, w_words, w_scales, r, out):
                 in_=y[g][:].rearrange("p t n -> p (t n)"),
             )
 
-        for g0 in range(0, G, 2):
-            for h in range(HALVES):
-                for g in (g0, g0 + 1):
-                    for t in range(PAIR):
-                        multiply(g, t, h)
-                        activate(g, t, h)
-                        add_residual(g, t, h)
-                    if h == HALVES - 1:
-                        store(g)
+        nc.gpsimd.memset(ws_raw[:].bitcast(I32), 0)
+        nc.vector.memset(zero[:], 0.0)
+        nc.scalar.activation(out=bias[:], in_=zero[:], func=GELU)
+        load_words()
+        load_x()
+        load_scales()
+        for g in range(G):
+            load_res(g)
+
+        deal_words()
+        interleave_vector(0, 256)
+        interleave_scalar(344, 512)
+        interleave_vector(256, 344)
+        interleave_scalar(736, 1024)
+        quantize(0, 256)
+        deal_scales()
+        quantize(256, 512)
+        interleave_vector(512, 736)
+        quantize(512, 1024)
+
+        first = [(g, t, 0) for g in range(G) for t in range(PAIR)]
+        order = first[: PAIR + 1]
+        for g in range(G):
+            order = order + [(g, t, 1) for t in range(PAIR)] + first[PAIR * (g + 1) + 1 : PAIR * (g + 2) + 1]
+        for g, t, h in order:
+            last = (t, h) == (PAIR - 1, HALVES - 1)
+            multiply(g, t, h)
+            finish(g, t, h, 2 if last else 1)
+            if last:
+                store(g)

@@ -60,8 +60,8 @@ def tile_rows_glin_gelu_res_kernel(tc, x, w_words, w_scales, r, out):
                 out=x_raw[:].rearrange("p j n -> p (j n)"), in_=x.rearrange("g (p j) n -> (g p) (j n)", j=PACK)
             )
 
-        def load_res(g):
-            nc.sync.dma_start(
+        def load_res(g, queue):
+            queue.dma_start(
                 out=res[g][:].rearrange("p t n -> p (t n)"),
                 in_=r[g].rearrange("(p t) n -> p (t n)", t=PAIR),
             )
@@ -111,15 +111,22 @@ def tile_rows_glin_gelu_res_kernel(tc, x, w_words, w_scales, r, out):
                 stop=True,
             )
 
-        def finish(g, t, h, pieces):
-            width = N_TILE // pieces
-            for at in range(0, N_TILE, width):
-                cols = slice(h * N_TILE + at, h * N_TILE + at + width)
-                nc.scalar.activation(out=y[g][:, t, cols], in_=acc[g][t][:, at : at + width], func=GELU, bias=bias[:])
+        def pieces(h):
+            width = N_TILE // (2 if h == HALVES - 1 else 1)
+            return [(at, at + width) for at in range(0, N_TILE, width)]
+
+        def activate(g, t, h):
+            for lo, hi in pieces(h):
+                cols = slice(h * N_TILE + lo, h * N_TILE + hi)
+                nc.scalar.activation(out=y[g][:, t, cols], in_=acc[g][t][:, lo:hi], func=GELU, bias=bias[:])
+
+        def add_residual(g, t, h):
+            for lo, hi in pieces(h):
+                cols = slice(h * N_TILE + lo, h * N_TILE + hi)
                 nc.vector.tensor_add(out=y[g][:, t, cols], in0=y[g][:, t, cols], in1=res[g][:, t, cols])
 
-        def store(g):
-            nc.sync.dma_start(
+        def store(g, queue):
+            queue.dma_start(
                 out=out[g].rearrange("(p t) n -> p (t n)", t=PAIR),
                 in_=y[g][:].rearrange("p t n -> p (t n)"),
             )
@@ -130,12 +137,14 @@ def tile_rows_glin_gelu_res_kernel(tc, x, w_words, w_scales, r, out):
         load_words()
         load_x()
         load_scales()
-        for g in range(G):
-            load_res(g)
+        load_res(0, nc.sync)
+        load_res(1, nc.sync)
 
         deal_words()
         interleave_vector(0, 256)
         interleave_scalar(344, 512)
+        load_res(2, nc.scalar)
+        load_res(3, nc.scalar)
         interleave_vector(256, 344)
         interleave_scalar(736, 1024)
         quantize(0, 256)
@@ -149,8 +158,10 @@ def tile_rows_glin_gelu_res_kernel(tc, x, w_words, w_scales, r, out):
         for g in range(G):
             order = order + [(g, t, 1) for t in range(PAIR)] + first[PAIR * (g + 1) + 1 : PAIR * (g + 2) + 1]
         for g, t, h in order:
-            last = (t, h) == (PAIR - 1, HALVES - 1)
             multiply(g, t, h)
-            finish(g, t, h, 2 if last else 1)
-            if last:
-                store(g)
+            activate(g, t, h)
+            if (t, h) == (PAIR - 1, HALVES - 1):
+                for half in range(HALVES):
+                    for tile in range(PAIR):
+                        add_residual(g, tile, half)
+                store(g, nc.scalar if g == G - 1 else nc.sync)

@@ -23,6 +23,8 @@ HALVES = N // N_TILE
 PAIR = M // P
 WORD_BYTES = 2
 RUN = 4
+BURST = 256
+PAGE = 4096
 
 
 def tile_rows_glin_gelu_res_kernel(tc, x, w_words, w_scales, r, out):
@@ -32,18 +34,18 @@ def tile_rows_glin_gelu_res_kernel(tc, x, w_words, w_scales, r, out):
         psum = ctx.enter_context(tc.psum_pool(name="psum", bufs=1))
         ctx.enter_context(tc.manual_schedule())
 
-        x_raw = sb.tile([P, PACK, N], F32)
+        x_raw = sb.tile([P, PACK, N], F32, align_bytes=PAGE)
         x_bf = sb.tile([P, N * PACK], BF16, align_bytes=64)
         x_codes = [sb.tile([P, N_TILE], U32, name="x_codes%d" % h, align_bytes=64) for h in range(HALVES)]
         x_scales = [sb.tile([P, N_TILE], U8, name="x_scales%d" % h, align_bytes=64) for h in range(HALVES)]
-        w_raw = sb.tile([P, M * WORD_BYTES], U8, align_bytes=64)
-        ws_raw = sb.tile([P, M], U8, align_bytes=64)
+        w_raw = sb.tile([P, M * WORD_BYTES], U8, align_bytes=BURST)
+        ws_raw = sb.tile([P, M], U8, align_bytes=BURST)
         w_dealt = sb.tile([P, M * WORD_BYTES], U8, align_bytes=64)
         ws_dealt = sb.tile([P, M], U8, align_bytes=64)
         zero = sb.tile([P, 1], F32)
         bias = sb.tile([P, 1], F32)
-        res = [sb.tile([P, PAIR, N], F32, name="res%d" % g) for g in range(G)]
-        y = [sb.tile([P, PAIR, N], F32, name="y%d" % g) for g in range(G)]
+        res = [sb.tile([P, PAIR, N], F32, name="res%d" % g, align_bytes=PAGE) for g in range(G)]
+        y = [sb.tile([P, PAIR, N], F32, name="y%d" % g, align_bytes=PAGE) for g in range(G)]
         acc = [[psum.tile([P, N_TILE], F32, name="acc%d_%d" % (g, t)) for t in range(PAIR)] for g in range(G)]
 
         def load_scales():

@@ -50,9 +50,12 @@ def tile_rows_glin_gelu_res_kernel(tc, x, w_words, w_scales, r, out):
 
         def load_scales():
             for g in range(G):
-                nc.sync.dma_start(
-                    out=ws_raw[ROWS * g : ROWS * g + BLOCKS, :].bitcast(I32), in_=w_scales[g].bitcast(I32)
-                )
+                step = BLOCKS if g < G // 2 else BLOCKS // 2
+                for f in range(0, BLOCKS, step):
+                    nc.sync.dma_start(
+                        out=ws_raw[ROWS * g + f : ROWS * g + f + step, :].bitcast(I32),
+                        in_=w_scales[g, f : f + step, :].bitcast(I32),
+                    )
 
         def load_words():
             nc.sync.dma_start(out=w_raw[:].bitcast(I32), in_=w_words.rearrange("g p b -> (g p) b").bitcast(I32))
@@ -139,14 +142,12 @@ def tile_rows_glin_gelu_res_kernel(tc, x, w_words, w_scales, r, out):
         load_words()
         load_x()
         load_scales()
-        load_res(0, nc.sync)
-        load_res(1, nc.sync)
+        for g in range(G):
+            load_res(g, nc.sync)
 
         deal_words()
         interleave_vector(0, 256)
         interleave_scalar(344, 512)
-        load_res(2, nc.scalar)
-        load_res(3, nc.scalar)
         interleave_vector(256, 344)
         interleave_scalar(736, 1024)
         quantize(0, 256)

@@ -167,4 +167,4 @@ def tile_rows_glin_gelu_res_kernel(tc, x, w_words, w_scales, r, out):
                 for half in range(HALVES):
                     for tile in range(PAIR):
                         add_residual(g, tile, half)
-                store(g, nc.scalar if g == G - 1 else nc.sync)
+                store(g, nc.sync)

@@ -21,10 +21,14 @@ BLOCKS = D // 32
 N_TILE = 512
 HALVES = N // N_TILE
 PAIR = M // P
-WORD_BYTES = 2
+W_WORD_BYTES = 2
+MX_ALIGN = 64
+DMA_ALIGN = 256
 RUN = 4
-BURST = 256
-PAGE = 4096
+VECTOR_SHARE = (344, 224)
+EARLY = 256
+LATE_PIECES = 2
+SPLIT_GROUPS = 2
 
 
 def tile_rows_glin_gelu_res_kernel(tc, x, w_words, w_scales, r, out):
@@ -34,28 +38,19 @@ def tile_rows_glin_gelu_res_kernel(tc, x, w_words, w_scales, r, out):
         psum = ctx.enter_context(tc.psum_pool(name="psum", bufs=1))
         ctx.enter_context(tc.manual_schedule())
 
-        x_raw = sb.tile([P, PACK, N], F32, align_bytes=PAGE)
-        x_bf = sb.tile([P, N * PACK], BF16, align_bytes=64)
-        x_codes = [sb.tile([P, N_TILE], U32, name="x_codes%d" % h, align_bytes=64) for h in range(HALVES)]
-        x_scales = [sb.tile([P, N_TILE], U8, name="x_scales%d" % h, align_bytes=64) for h in range(HALVES)]
-        w_raw = sb.tile([P, M * WORD_BYTES], U8, align_bytes=BURST)
-        ws_raw = sb.tile([P, M], U8, align_bytes=BURST)
-        w_dealt = sb.tile([P, M * WORD_BYTES], U8, align_bytes=64)
-        ws_dealt = sb.tile([P, M], U8, align_bytes=64)
+        x_raw = sb.tile([P, PACK, N], F32, align_bytes=DMA_ALIGN)
+        x_bf = sb.tile([P, N * PACK], BF16, align_bytes=MX_ALIGN)
+        x_codes = [sb.tile([P, N_TILE], U32, name="x_codes%d" % h, align_bytes=MX_ALIGN) for h in range(HALVES)]
+        x_scales = [sb.tile([P, N_TILE], U8, name="x_scales%d" % h, align_bytes=MX_ALIGN) for h in range(HALVES)]
+        w_raw = sb.tile([P, M * W_WORD_BYTES], U8, align_bytes=DMA_ALIGN)
+        ws_raw = sb.tile([P, M], U8, align_bytes=DMA_ALIGN)
+        w_dealt = sb.tile([P, M * W_WORD_BYTES], U8, align_bytes=MX_ALIGN)
+        ws_dealt = sb.tile([P, M], U8, align_bytes=MX_ALIGN)
         zero = sb.tile([P, 1], F32)
         bias = sb.tile([P, 1], F32)
-        res = [sb.tile([P, PAIR, N], F32, name="res%d" % g, align_bytes=PAGE) for g in range(G)]
-        y = [sb.tile([P, PAIR, N], F32, name="y%d" % g, align_bytes=PAGE) for g in range(G)]
+        res = [sb.tile([P, PAIR, N], F32, name="res%d" % g, align_bytes=DMA_ALIGN) for g in range(G)]
+        y = [sb.tile([P, PAIR, N], F32, name="y%d" % g, align_bytes=DMA_ALIGN) for g in range(G)]
         acc = [[psum.tile([P, N_TILE], F32, name="acc%d_%d" % (g, t)) for t in range(PAIR)] for g in range(G)]
-
-        def load_scales():
-            for g in range(G):
-                step = BLOCKS if g < G // 2 else BLOCKS // 2
-                for f in range(0, BLOCKS, step):
-                    nc.sync.dma_start(
-                        out=ws_raw[ROWS * g + f : ROWS * g + f + step, :].bitcast(I32),
-                        in_=w_scales[g, f : f + step, :].bitcast(I32),
-                    )
 
         def load_words():
             nc.sync.dma_start(out=w_raw[:].bitcast(I32), in_=w_words.rearrange("g p b -> (g p) b").bitcast(I32))
@@ -65,23 +60,31 @@ def tile_rows_glin_gelu_res_kernel(tc, x, w_words, w_scales, r, out):
                 out=x_raw[:].rearrange("p j n -> p (j n)"), in_=x.rearrange("g (p j) n -> (g p) (j n)", j=PACK)
             )
 
-        def load_res(g, queue):
-            queue.dma_start(
+        def load_scales(g):
+            step = BLOCKS if g < G - SPLIT_GROUPS else BLOCKS // 2
+            for f in range(0, BLOCKS, step):
+                nc.sync.dma_start(
+                    out=ws_raw[ROWS * g + f : ROWS * g + f + step, :].bitcast(I32),
+                    in_=w_scales[g, f : f + step, :].bitcast(I32),
+                )
+
+        def load_residual(g):
+            nc.sync.dma_start(
                 out=res[g][:].rearrange("p t n -> p (t n)"),
                 in_=r[g].rearrange("(p t) n -> p (t n)", t=PAIR),
             )
 
-        def views(lo, hi):
+        def interleave_views(lo, hi):
             target = x_bf[:, lo * PACK : hi * PACK].rearrange("p (c i j) -> p c j i", i=RUN, j=PACK)
             source = x_raw[:, :, lo:hi].rearrange("p j (c i) -> p c j i", i=RUN)
             return target, source
 
         def interleave_vector(lo, hi):
-            target, source = views(lo, hi)
+            target, source = interleave_views(lo, hi)
             nc.vector.tensor_copy(out=target, in_=source)
 
         def interleave_scalar(lo, hi):
-            target, source = views(lo, hi)
+            target, source = interleave_views(lo, hi)
             nc.scalar.copy(out=target, in_=source)
 
         def quantize(lo, hi):
@@ -94,21 +97,21 @@ def tile_rows_glin_gelu_res_kernel(tc, x, w_words, w_scales, r, out):
 
         def deal_words():
             nc.vector.tensor_copy(
-                out=w_dealt[:].rearrange("p (t m b) -> p t m b", t=PAIR, b=WORD_BYTES),
-                in_=w_raw[:].rearrange("p (m t b) -> p t m b", t=PAIR, b=WORD_BYTES),
+                out=w_dealt[:].rearrange("p (t q b) -> p t q b", t=PAIR, b=W_WORD_BYTES),
+                in_=w_raw[:].rearrange("p (q t b) -> p t q b", t=PAIR, b=W_WORD_BYTES),
             )
 
         def deal_scales():
             nc.vector.tensor_copy(
-                out=ws_dealt[:].rearrange("p (t m) -> p t m", t=PAIR),
-                in_=ws_raw[:].rearrange("p (m t) -> p t m", t=PAIR),
+                out=ws_dealt[:].rearrange("p (t q) -> p t q", t=PAIR),
+                in_=ws_raw[:].rearrange("p (q t) -> p t q", t=PAIR),
             )
 
         def multiply(g, t, h):
             rows = slice(ROWS * g, ROWS * (g + 1))
             nc.tensor.matmul_mx(
                 out=acc[g][t][:],
-                lhsT=w_dealt[rows, t * P * WORD_BYTES : (t + 1) * P * WORD_BYTES].bitcast(FP4X4),
+                lhsT=w_dealt[rows, t * P * W_WORD_BYTES : (t + 1) * P * W_WORD_BYTES].bitcast(FP4X4),
                 lhsT_scale=ws_dealt[rows, t * P : (t + 1) * P],
                 rhs=x_codes[h][rows, :].bitcast(FP8X4),
                 rhs_scale=x_scales[h][rows, :],
@@ -117,7 +120,7 @@ def tile_rows_glin_gelu_res_kernel(tc, x, w_words, w_scales, r, out):
             )
 
         def pieces(h):
-            width = N_TILE // (2 if h == HALVES - 1 else 1)
+            width = N_TILE // (LATE_PIECES if h == HALVES - 1 else 1)
             return [(at, at + width) for at in range(0, N_TILE, width)]
 
         def activate(g, t, h):
@@ -130,8 +133,8 @@ def tile_rows_glin_gelu_res_kernel(tc, x, w_words, w_scales, r, out):
                 cols = slice(h * N_TILE + lo, h * N_TILE + hi)
                 nc.vector.tensor_add(out=y[g][:, t, cols], in0=y[g][:, t, cols], in1=res[g][:, t, cols])
 
-        def store(g, queue):
-            queue.dma_start(
+        def store(g):
+            nc.sync.dma_start(
                 out=out[g].rearrange("(p t) n -> p (t n)", t=PAIR),
                 in_=y[g][:].rearrange("p t n -> p (t n)"),
             )
@@ -139,22 +142,26 @@ def tile_rows_glin_gelu_res_kernel(tc, x, w_words, w_scales, r, out):
         nc.gpsimd.memset(ws_raw[:].bitcast(I32), 0)
         nc.vector.memset(zero[:], 0.0)
         nc.scalar.activation(out=bias[:], in_=zero[:], func=GELU)
+
         load_words()
         load_x()
-        load_scales()
         for g in range(G):
-            load_res(g, nc.sync)
+            load_scales(g)
+        for g in range(G):
+            load_residual(g)
 
+        cut_first = VECTOR_SHARE[0]
+        cut_second = N_TILE + VECTOR_SHARE[1]
         deal_words()
-        interleave_vector(0, 256)
-        interleave_scalar(344, 512)
-        interleave_vector(256, 344)
-        interleave_scalar(736, 1024)
-        quantize(0, 256)
+        interleave_vector(0, EARLY)
+        interleave_scalar(cut_first, N_TILE)
+        interleave_vector(EARLY, cut_first)
+        interleave_scalar(cut_second, N)
+        quantize(0, EARLY)
         deal_scales()
-        quantize(256, 512)
-        interleave_vector(512, 736)
-        quantize(512, 1024)
+        quantize(EARLY, N_TILE)
+        interleave_vector(N_TILE, cut_second)
+        quantize(N_TILE, N)
 
         first = [(g, t, 0) for g in range(G) for t in range(PAIR)]
         order = first[: PAIR + 1]
@@ -167,4 +174,4 @@ def tile_rows_glin_gelu_res_kernel(tc, x, w_words, w_scales, r, out):
                 for half in range(HALVES):
                     for tile in range(PAIR):
                         add_residual(g, tile, half)
-                store(g, nc.sync)
+                store(g)

@@ -28,7 +28,6 @@ RUN = 4
 VECTOR_SHARE = (344, 224)
 EARLY = 256
 LATE_PIECES = 2
-SPLIT_GROUPS = 2
 
 
 def tile_rows_glin_gelu_res_kernel(tc, x, w_words, w_scales, r, out):
@@ -61,12 +60,9 @@ def tile_rows_glin_gelu_res_kernel(tc, x, w_words, w_scales, r, out):
             )
 
         def load_scales(g):
-            step = BLOCKS if g < G - SPLIT_GROUPS else BLOCKS // 2
-            for f in range(0, BLOCKS, step):
-                nc.sync.dma_start(
-                    out=ws_raw[ROWS * g + f : ROWS * g + f + step, :].bitcast(I32),
-                    in_=w_scales[g, f : f + step, :].bitcast(I32),
-                )
+            nc.sync.dma_start(
+                out=ws_raw[ROWS * g : ROWS * g + BLOCKS, :].bitcast(I32), in_=w_scales[g].bitcast(I32)
+            )
 
         def load_residual(g):
             nc.sync.dma_start(
@@ -143,8 +139,8 @@ def tile_rows_glin_gelu_res_kernel(tc, x, w_words, w_scales, r, out):
         nc.vector.memset(zero[:], 0.0)
         nc.scalar.activation(out=bias[:], in_=zero[:], func=GELU)
 
-        load_words()
         load_x()
+        load_words()
         for g in range(G):
             load_scales(g)
         for g in range(G):
@@ -152,11 +148,11 @@ def tile_rows_glin_gelu_res_kernel(tc, x, w_words, w_scales, r, out):
 
         cut_first = VECTOR_SHARE[0]
         cut_second = N_TILE + VECTOR_SHARE[1]
-        deal_words()
         interleave_vector(0, EARLY)
         interleave_scalar(cut_first, N_TILE)
         interleave_vector(EARLY, cut_first)
         interleave_scalar(cut_second, N)
+        deal_words()
         quantize(0, EARLY)
         deal_scales()
         quantize(EARLY, N_TILE)

@@ -27,6 +27,7 @@ DMA_ALIGN = 256
 RUN = 4
 VECTOR_SHARE = (344, 224)
 EARLY = 256
+SETS = 2
 LATE_PIECES = 2
 
 
@@ -42,9 +43,9 @@ def tile_rows_glin_gelu_res_kernel(tc, x, w_words, w_scales, r, out):
         x_codes = [sb.tile([P, N_TILE], U32, name="x_codes%d" % h, align_bytes=MX_ALIGN) for h in range(HALVES)]
         x_scales = [sb.tile([P, N_TILE], U8, name="x_scales%d" % h, align_bytes=MX_ALIGN) for h in range(HALVES)]
         w_raw = sb.tile([P, M * W_WORD_BYTES], U8, align_bytes=DMA_ALIGN)
-        ws_raw = sb.tile([P, M], U8, align_bytes=DMA_ALIGN)
+        ws_raw = sb.tile([P, SETS, M], U8, align_bytes=DMA_ALIGN)
         w_dealt = sb.tile([P, M * W_WORD_BYTES], U8, align_bytes=MX_ALIGN)
-        ws_dealt = sb.tile([P, M], U8, align_bytes=MX_ALIGN)
+        ws_dealt = sb.tile([P, SETS, M], U8, align_bytes=MX_ALIGN)
         zero = sb.tile([P, 1], F32)
         bias = sb.tile([P, 1], F32)
         res = [sb.tile([P, PAIR, N], F32, name="res%d" % g, align_bytes=DMA_ALIGN) for g in range(G)]
@@ -60,9 +61,13 @@ def tile_rows_glin_gelu_res_kernel(tc, x, w_words, w_scales, r, out):
             )
 
         def load_scales(g):
-            nc.sync.dma_start(
-                out=ws_raw[ROWS * g : ROWS * g + BLOCKS, :].bitcast(I32), in_=w_scales[g].bitcast(I32)
-            )
+            s = g * SETS // G
+            step = BLOCKS // (1 + s)
+            for f in range(0, BLOCKS, step):
+                nc.sync.dma_start(
+                    out=ws_raw[ROWS * g + f : ROWS * g + f + step, s, :].bitcast(I32),
+                    in_=w_scales[g, f : f + step, :].bitcast(I32),
+                )
 
         def load_residual(g):
             nc.sync.dma_start(
@@ -97,10 +102,10 @@ def tile_rows_glin_gelu_res_kernel(tc, x, w_words, w_scales, r, out):
                 in_=w_raw[:].rearrange("p (q t b) -> p t q b", t=PAIR, b=W_WORD_BYTES),
             )
 
-        def deal_scales():
+        def deal_scales(s):
             nc.vector.tensor_copy(
-                out=ws_dealt[:].rearrange("p (t q) -> p t q", t=PAIR),
-                in_=ws_raw[:].rearrange("p (q t) -> p t q", t=PAIR),
+                out=ws_dealt[:, s, :].rearrange("p (t q) -> p t q", t=PAIR),
+                in_=ws_raw[:, s, :].rearrange("p (q t) -> p t q", t=PAIR),
             )
 
         def multiply(g, t, h):
@@ -108,7 +113,7 @@ def tile_rows_glin_gelu_res_kernel(tc, x, w_words, w_scales, r, out):
             nc.tensor.matmul_mx(
                 out=acc[g][t][:],
                 lhsT=w_dealt[rows, t * P * W_WORD_BYTES : (t + 1) * P * W_WORD_BYTES].bitcast(FP4X4),
-                lhsT_scale=ws_dealt[rows, t * P : (t + 1) * P],
+                lhsT_scale=ws_dealt[rows, g * SETS // G, t * P : (t + 1) * P],
                 rhs=x_codes[h][rows, :].bitcast(FP8X4),
                 rhs_scale=x_scales[h][rows, :],
                 start=True,
@@ -135,15 +140,18 @@ def tile_rows_glin_gelu_res_kernel(tc, x, w_words, w_scales, r, out):
                 in_=y[g][:].rearrange("p t n -> p (t n)"),
             )
 
-        nc.gpsimd.memset(ws_raw[:].bitcast(I32), 0)
+        nc.gpsimd.memset(ws_raw[:].rearrange("p s m -> p (s m)").bitcast(I32), 0)
         nc.vector.memset(zero[:], 0.0)
         nc.scalar.activation(out=bias[:], in_=zero[:], func=GELU)
 
         load_x()
         load_words()
-        for g in range(G):
+        for g in range(G // SETS):
             load_scales(g)
-        for g in range(G):
+        load_residual(0)
+        for g in range(G // SETS, G):
+            load_scales(g)
+        for g in range(1, G):
             load_residual(g)
 
         cut_first = VECTOR_SHARE[0]
@@ -154,10 +162,11 @@ def tile_rows_glin_gelu_res_kernel(tc, x, w_words, w_scales, r, out):
         interleave_scalar(cut_second, N)
         deal_words()
         quantize(0, EARLY)
-        deal_scales()
+        deal_scales(0)
         quantize(EARLY, N_TILE)
         interleave_vector(N_TILE, cut_second)
         quantize(N_TILE, N)
+        deal_scales(1)
 
         first = [(g, t, 0) for g in range(G) for t in range(PAIR)]
         order = first[: PAIR + 1]

@@ -48,7 +48,9 @@ def tile_rows_glin_gelu_res_kernel(tc, x, w_words, w_scales, r, out):
         ws_dealt = sb.tile([P, SETS, M], U8, align_bytes=MX_ALIGN)
         zero = sb.tile([P, 1], F32)
         bias = sb.tile([P, 1], F32)
-        res = [sb.tile([P, PAIR, N], F32, name="res%d" % g, align_bytes=DMA_ALIGN) for g in range(G)]
+        res = [
+            sb.tile([P, G // SETS, PAIR, N], F32, name="res%d" % s, align_bytes=DMA_ALIGN) for s in range(SETS)
+        ]
         y = [sb.tile([P, PAIR, N], F32, name="y%d" % g, align_bytes=DMA_ALIGN) for g in range(G)]
         acc = [[psum.tile([P, N_TILE], F32, name="acc%d_%d" % (g, t)) for t in range(PAIR)] for g in range(G)]
 
@@ -62,17 +64,18 @@ def tile_rows_glin_gelu_res_kernel(tc, x, w_words, w_scales, r, out):
 
         def load_scales(g):
             s = g * SETS // G
-            step = BLOCKS // (1 + s)
+            step = BLOCKS // 2
             for f in range(0, BLOCKS, step):
                 nc.sync.dma_start(
                     out=ws_raw[ROWS * g + f : ROWS * g + f + step, s, :].bitcast(I32),
                     in_=w_scales[g, f : f + step, :].bitcast(I32),
                 )
 
-        def load_residual(g):
+        def load_residuals(s):
+            groups = slice(s * G // SETS, (s + 1) * G // SETS)
             nc.sync.dma_start(
-                out=res[g][:].rearrange("p t n -> p (t n)"),
-                in_=r[g].rearrange("(p t) n -> p (t n)", t=PAIR),
+                out=res[s][:].rearrange("p g t n -> p g (t n)"),
+                in_=r[groups].rearrange("g (p t) n -> p g (t n)", t=PAIR),
             )
 
         def interleave_views(lo, hi):
@@ -132,7 +135,7 @@ def tile_rows_glin_gelu_res_kernel(tc, x, w_words, w_scales, r, out):
         def add_residual(g, t, h):
             for lo, hi in pieces(h):
                 cols = slice(h * N_TILE + lo, h * N_TILE + hi)
-                nc.vector.tensor_add(out=y[g][:, t, cols], in0=y[g][:, t, cols], in1=res[g][:, t, cols])
+                nc.vector.tensor_add(out=y[g][:, t, cols], in0=y[g][:, t, cols], in1=res[g * SETS // G][:, g % (G // SETS), t, cols])
 
         def store(g):
             nc.sync.dma_start(
@@ -148,11 +151,10 @@ def tile_rows_glin_gelu_res_kernel(tc, x, w_words, w_scales, r, out):
         load_words()
         for g in range(G // SETS):
             load_scales(g)
-        load_residual(0)
+        load_residuals(0)
         for g in range(G // SETS, G):
             load_scales(g)
-        for g in range(1, G):
-            load_residual(g)
+        load_residuals(1)
 
         cut_first = VECTOR_SHARE[0]
         cut_second = N_TILE + VECTOR_SHARE[1]
@@ -166,7 +168,6 @@ def tile_rows_glin_gelu_res_kernel(tc, x, w_words, w_scales, r, out):
         quantize(EARLY, N_TILE)
         interleave_vector(N_TILE, cut_second)
         quantize(N_TILE, N)
-        deal_scales(1)
 
         first = [(g, t, 0) for g in range(G) for t in range(PAIR)]
         order = first[: PAIR + 1]
@@ -179,4 +180,6 @@ def tile_rows_glin_gelu_res_kernel(tc, x, w_words, w_scales, r, out):
                 for half in range(HALVES):
                     for tile in range(PAIR):
                         add_residual(g, tile, half)
+                        if (g, tile, half) == (0, 0, 0):
+                            deal_scales(1)
                 store(g)

@@ -54,6 +54,9 @@ def tile_rows_glin_gelu_res_kernel(tc, x, w_words, w_scales, r, out):
         y = [sb.tile([P, PAIR, N], F32, name="y%d" % g, align_bytes=DMA_ALIGN) for g in range(G)]
         acc = [[psum.tile([P, N_TILE], F32, name="acc%d_%d" % (g, t)) for t in range(PAIR)] for g in range(G)]
 
+        def scale_set(g):
+            return 1 if g == G - 1 else 0
+
         def load_words():
             nc.sync.dma_start(out=w_raw[:].bitcast(I32), in_=w_words.rearrange("g p b -> (g p) b").bitcast(I32))
 
@@ -62,14 +65,13 @@ def tile_rows_glin_gelu_res_kernel(tc, x, w_words, w_scales, r, out):
                 out=x_raw[:].rearrange("p j n -> p (j n)"), in_=x.rearrange("g (p j) n -> (g p) (j n)", j=PACK)
             )
 
-        def load_scales(g):
-            s = g * SETS // G
-            step = BLOCKS // 2
-            for f in range(0, BLOCKS, step):
-                nc.sync.dma_start(
-                    out=ws_raw[ROWS * g + f : ROWS * g + f + step, s, :].bitcast(I32),
-                    in_=w_scales[g, f : f + step, :].bitcast(I32),
-                )
+        def load_scales(g, rows, width):
+            for f in range(0, BLOCKS, rows):
+                for at in range(0, M, width):
+                    nc.sync.dma_start(
+                        out=ws_raw[ROWS * g + f : ROWS * g + f + rows, scale_set(g), at : at + width].bitcast(I32),
+                        in_=w_scales[g, f : f + rows, at : at + width].bitcast(I32),
+                    )
 
         def load_residuals(s):
             groups = slice(s * G // SETS, (s + 1) * G // SETS)
@@ -116,7 +118,7 @@ def tile_rows_glin_gelu_res_kernel(tc, x, w_words, w_scales, r, out):
             nc.tensor.matmul_mx(
                 out=acc[g][t][:],
                 lhsT=w_dealt[rows, t * P * W_WORD_BYTES : (t + 1) * P * W_WORD_BYTES].bitcast(FP4X4),
-                lhsT_scale=ws_dealt[rows, g * SETS // G, t * P : (t + 1) * P],
+                lhsT_scale=ws_dealt[rows, scale_set(g), t * P : (t + 1) * P],
                 rhs=x_codes[h][rows, :].bitcast(FP8X4),
                 rhs_scale=x_scales[h][rows, :],
                 start=True,
@@ -149,11 +151,10 @@ def tile_rows_glin_gelu_res_kernel(tc, x, w_words, w_scales, r, out):
 
         load_x()
         load_words()
-        for g in range(G // SETS):
-            load_scales(g)
+        for g in range(G - 1):
+            load_scales(g, BLOCKS // 2 if g == 0 else BLOCKS, M)
         load_residuals(0)
-        for g in range(G // SETS, G):
-            load_scales(g)
+        load_scales(G - 1, BLOCKS // 2, M // 2)
         load_residuals(1)
 
         cut_first = VECTOR_SHARE[0]
@@ -180,6 +181,6 @@ def tile_rows_glin_gelu_res_kernel(tc, x, w_words, w_scales, r, out):
                 for half in range(HALVES):
                     for tile in range(PAIR):
                         add_residual(g, tile, half)
-                        if (g, tile, half) == (0, 0, 0):
-                            deal_scales(1)
                 store(g)
+                if g == 0:
+                    deal_scales(1)

from contextlib import ExitStack

import concourse.mybir as mybir

G, D, M, N = 4, 128, 256, 1024
FLOPS = 2 * G * D * M * N

F32 = mybir.dt.float32
BF16 = mybir.dt.bfloat16
I32 = mybir.dt.int32
U32 = mybir.dt.uint32
U8 = mybir.dt.uint8
FP8X4 = mybir.dt.float8_e4m3fn_x4
FP4X4 = mybir.dt.float4_e2m1fn_x4
GELU = mybir.ActivationFunctionType.Gelu_apprx_tanh

P = 128
PACK = 4
ROWS = D // PACK
BLOCKS = D // 32
N_TILE = 512
HALVES = N // N_TILE
PAIR = M // P
W_WORD_BYTES = 2
MX_ALIGN = 64
DMA_ALIGN = 256
RUN = 4
VECTOR_SHARE = (344, 224)
EARLY = 256
SETS = 2
LATE_PIECES = 2


def tile_rows_glin_gelu_res_kernel(tc, x, w_words, w_scales, r, out):
    nc = tc.nc
    with ExitStack() as ctx:
        sb = ctx.enter_context(tc.tile_pool(name="sb", bufs=1))
        psum = ctx.enter_context(tc.psum_pool(name="psum", bufs=1))
        ctx.enter_context(tc.manual_schedule())

        x_raw = sb.tile([P, PACK, N], F32, align_bytes=DMA_ALIGN)
        x_bf = sb.tile([P, N * PACK], BF16, align_bytes=MX_ALIGN)
        x_codes = [sb.tile([P, N_TILE], U32, name="x_codes%d" % h, align_bytes=MX_ALIGN) for h in range(HALVES)]
        x_scales = [sb.tile([P, N_TILE], U8, name="x_scales%d" % h, align_bytes=MX_ALIGN) for h in range(HALVES)]
        w_raw = sb.tile([P, M * W_WORD_BYTES], U8, align_bytes=DMA_ALIGN)
        ws_raw = sb.tile([P, SETS, M], U8, align_bytes=DMA_ALIGN)
        w_dealt = sb.tile([P, M * W_WORD_BYTES], U8, align_bytes=MX_ALIGN)
        ws_dealt = sb.tile([P, SETS, M], U8, align_bytes=MX_ALIGN)
        zero = sb.tile([P, 1], F32)
        bias = sb.tile([P, 1], F32)
        res = [
            sb.tile([P, G // SETS, PAIR, N], F32, name="res%d" % s, align_bytes=DMA_ALIGN) for s in range(SETS)
        ]
        y = [sb.tile([P, PAIR, N], F32, name="y%d" % g, align_bytes=DMA_ALIGN) for g in range(G)]
        acc = [[psum.tile([P, N_TILE], F32, name="acc%d_%d" % (g, t)) for t in range(PAIR)] for g in range(G)]

        def scale_set(g):
            return 1 if g == G - 1 else 0

        def load_words():
            nc.sync.dma_start(out=w_raw[:].bitcast(I32), in_=w_words.rearrange("g p b -> (g p) b").bitcast(I32))

        def load_x():
            nc.sync.dma_start(
                out=x_raw[:].rearrange("p j n -> p (j n)"), in_=x.rearrange("g (p j) n -> (g p) (j n)", j=PACK)
            )

        def load_scales(g, rows, width):
            for f in range(0, BLOCKS, rows):
                for at in range(0, M, width):
                    nc.sync.dma_start(
                        out=ws_raw[ROWS * g + f : ROWS * g + f + rows, scale_set(g), at : at + width].bitcast(I32),
                        in_=w_scales[g, f : f + rows, at : at + width].bitcast(I32),
                    )

        def load_residuals(s):
            groups = slice(s * G // SETS, (s + 1) * G // SETS)
            nc.sync.dma_start(
                out=res[s][:].rearrange("p g t n -> p g (t n)"),
                in_=r[groups].rearrange("g (p t) n -> p g (t n)", t=PAIR),
            )

        def interleave_views(lo, hi):
            target = x_bf[:, lo * PACK : hi * PACK].rearrange("p (c i j) -> p c j i", i=RUN, j=PACK)
            source = x_raw[:, :, lo:hi].rearrange("p j (c i) -> p c j i", i=RUN)
            return target, source

        def interleave_vector(lo, hi):
            target, source = interleave_views(lo, hi)
            nc.vector.tensor_copy(out=target, in_=source)

        def interleave_scalar(lo, hi):
            target, source = interleave_views(lo, hi)
            nc.scalar.copy(out=target, in_=source)

        def quantize(lo, hi):
            h, at = divmod(lo, N_TILE)
            nc.vector.quantize_mx(
                out=x_codes[h][:, at : at + hi - lo].bitcast(FP8X4),
                scales=x_scales[h][:, at : at + hi - lo],
                in_=x_bf[:, lo * PACK : hi * PACK],
            )

        def deal_words():
            nc.vector.tensor_copy(
                out=w_dealt[:].rearrange("p (t q b) -> p t q b", t=PAIR, b=W_WORD_BYTES),
                in_=w_raw[:].rearrange("p (q t b) -> p t q b", t=PAIR, b=W_WORD_BYTES),
            )

        def deal_scales(s):
            nc.vector.tensor_copy(
                out=ws_dealt[:, s, :].rearrange("p (t q) -> p t q", t=PAIR),
                in_=ws_raw[:, s, :].rearrange("p (q t) -> p t q", t=PAIR),
            )

        def multiply(g, t, h):
            rows = slice(ROWS * g, ROWS * (g + 1))
            nc.tensor.matmul_mx(
                out=acc[g][t][:],
                lhsT=w_dealt[rows, t * P * W_WORD_BYTES : (t + 1) * P * W_WORD_BYTES].bitcast(FP4X4),
                lhsT_scale=ws_dealt[rows, scale_set(g), t * P : (t + 1) * P],
                rhs=x_codes[h][rows, :].bitcast(FP8X4),
                rhs_scale=x_scales[h][rows, :],
                start=True,
                stop=True,
            )

        def pieces(h):
            width = N_TILE // (LATE_PIECES if h == HALVES - 1 else 1)
            return [(at, at + width) for at in range(0, N_TILE, width)]

        def activate(g, t, h):
            for lo, hi in pieces(h):
                cols = slice(h * N_TILE + lo, h * N_TILE + hi)
                nc.scalar.activation(out=y[g][:, t, cols], in_=acc[g][t][:, lo:hi], func=GELU, bias=bias[:])

        def add_residual(g, t, h):
            for lo, hi in pieces(h):
                cols = slice(h * N_TILE + lo, h * N_TILE + hi)
                nc.vector.tensor_add(out=y[g][:, t, cols], in0=y[g][:, t, cols], in1=res[g * SETS // G][:, g % (G // SETS), t, cols])

        def store(g):
            nc.sync.dma_start(
                out=out[g].rearrange("(p t) n -> p (t n)", t=PAIR),
                in_=y[g][:].rearrange("p t n -> p (t n)"),
            )

        nc.gpsimd.memset(ws_raw[:].rearrange("p s m -> p (s m)").bitcast(I32), 0)
        nc.vector.memset(zero[:], 0.0)
        nc.scalar.activation(out=bias[:], in_=zero[:], func=GELU)

        load_x()
        load_words()
        for g in range(G - 1):
            load_scales(g, BLOCKS // 2 if g == 0 else BLOCKS, M)
        load_residuals(0)
        load_scales(G - 1, BLOCKS // 2, M // 2)
        load_residuals(1)

        cut_first = VECTOR_SHARE[0]
        cut_second = N_TILE + VECTOR_SHARE[1]
        interleave_vector(0, EARLY)
        interleave_scalar(cut_first, N_TILE)
        interleave_vector(EARLY, cut_first)
        interleave_scalar(cut_second, N)
        deal_words()
        quantize(0, EARLY)
        deal_scales(0)
        quantize(EARLY, N_TILE)
        interleave_vector(N_TILE, cut_second)
        quantize(N_TILE, N)

        first = [(g, t, 0) for g in range(G) for t in range(PAIR)]
        order = first[: PAIR + 1]
        for g in range(G):
            order = order + [(g, t, 1) for t in range(PAIR)] + first[PAIR * (g + 1) + 1 : PAIR * (g + 2) + 1]
        for g, t, h in order:
            multiply(g, t, h)
            activate(g, t, h)
            if (t, h) == (PAIR - 1, HALVES - 1):
                for half in range(HALVES):
                    for tile in range(PAIR):
                        add_residual(g, tile, half)
                store(g)
                if g == 0:
                    deal_scales(1)
